import numpy as np
import ml_dtypes


def mxq(x, axis, fmt="e4m3"):
    dtype, down = {"e4m3": (ml_dtypes.float8_e4m3fn, 7), "e5m2": (ml_dtypes.float8_e5m2, 14)}[fmt]
    v = np.moveaxis(np.asarray(x, np.float32).astype(ml_dtypes.bfloat16).astype(np.float64), axis, -1)
    blocks = v.reshape(v.shape[:-1] + (-1, 32))
    amax = np.abs(blocks).max(-1, keepdims=True)
    byte = np.maximum(np.where(amax > 0, np.frexp(amax)[1] - 1 + 127, 0) - down, 1)
    scale = np.exp2(byte - 127.0)
    codes = (blocks / scale).astype(np.float32).astype(dtype).astype(np.float64)
    return np.moveaxis((codes * scale).reshape(v.shape), -1, axis)


WIDE = False


def mx_kscale(k):
    if not WIDE:
        return np.ones(k)
    levels = np.array([10, -10, 5, -5, 0])
    if k % 512:
        return np.exp2(np.random.permutation(np.resize(levels, k // 32))).repeat(32)
    a = np.empty((k // 512, 16))
    for p in range(k // 512):
        a[p, :8] = np.random.permutation(np.resize(levels, 8))
        for g in range(8):
            far = levels[np.abs(levels - a[p, g]) >= 10]
            a[p, g + 8] = far[np.random.randint(len(far))]
    return np.exp2(a.ravel()).repeat(32)


def f64(x):
    return np.asarray(x).astype(np.float64)


def striped(idx):
    return np.tile(idx.reshape(-1, 16).T, (8, 1)).astype(np.uint16)


def unstriped(offs):
    return offs[:16].T.reshape(-1).astype(np.int64)


def striped8(idx):
    return np.concatenate([x.reshape(-1, 16).T for x in idx]).astype(np.uint16)


def runs(offs, k):
    lists = np.stack([offs[16 * r : 16 * r + 16].T.reshape(-1) for r in range(8)]).astype(np.int64)
    return lists[np.arange(k) % 512 // 64]


def pack_weight(w):
    k, n = w.shape
    w = f64(np.asarray(w, np.float32).astype(ml_dtypes.bfloat16)).reshape(k // 32, 32, n)
    amax = np.abs(w).max(1)
    byte = np.clip(np.where(amax > 0, np.frexp(amax)[1] - 1 + 127 - 7, 1), 1, 254)
    scaled = (w * np.exp2(127.0 - byte)[:, None, :]).reshape(k, n).astype(np.float32)
    words = np.ascontiguousarray(scaled.reshape(k // 512, 128, 4, n).transpose(0, 1, 3, 2)).astype(ml_dtypes.float8_e4m3fn).view(np.uint8)
    return words, np.ascontiguousarray(byte.astype(np.uint8).reshape(k // 512, 16, n))


def unpack_weight(words, scales):
    g, p, n, _ = words.shape
    vals = np.ascontiguousarray(words).view(ml_dtypes.float8_e4m3fn).astype(np.float64) * np.repeat(np.exp2(scales.astype(np.float64) - 127.0), 8, axis=1)[..., None]
    return vals.transpose(0, 1, 3, 2).reshape(g * 512, n)


def sigmoid(v):
    return 1.0 / (1.0 + np.exp(-np.maximum(v, -700.0)))


K, T, S, N, G, H, W = 512, 2048, 512, 512, 2048, 512, 384


def setup_inputs():
    n = np.random.standard_normal
    s = mx_kscale(K)[:, None]
    u = mx_kscale(S)
    packed_xT = pack_weight(n((K, T)) * s)
    packed_dT = pack_weight(n((K, G)) / s)
    return {
        "x_words": packed_xT[0],
        "x_scales": packed_xT[1],
        "d_words": packed_dT[0],
        "d_scales": packed_dT[1],
        "gn": (np.random.uniform(0.5, 1.5, (H, 1)) * u[:, None]).astype(np.float32),
        "w1": (n((H, N)) / np.sqrt(H) / u[:, None]).astype(np.float32),
        "sl": np.random.uniform(1.0, 2.0, (N, 1)).astype(np.float32),
        "th": (0.5 * n((N, 1))).astype(np.float32),
        "offs": striped(np.random.permutation(T)[:S]),
        "k1": striped8(np.random.randint(0, G, (8, H))),
        "n1": striped(np.random.permutation(S)[:W]),
        "n2": striped(np.random.permutation(S)[:W]),
        "n3": striped(np.random.permutation(S)),
        "n4": striped(np.random.permutation(S)),
    }


def reference(x_words, x_scales, d_words, d_scales, gn, w1, sl, th, offs, k1, n1, n2, n3, n4):
    d_k1 = unpack_weight(d_words, d_scales)[np.arange(K)[:, None], runs(k1, K)]
    xq = unpack_weight(x_words, x_scales)[:, unstriped(offs)]
    h = 0.0625 * (d_k1.T @ xq)
    old = h[:, unstriped(n1)]
    pa = h[:, unstriped(n2)]
    ra = old / (np.abs(pa) + 0.5)
    ds = h.copy()
    ds[:, unstriped(n1)] = ra
    z = f64(gn) * ds
    h2 = mxq(f64(w1), 0, "e4m3").T @ mxq(z, 0, "e4m3")
    st = h2 - h2[:, unstriped(n3)]
    sg = sigmoid(f64(sl) * (st[:, unstriped(n4)] - f64(th)))
    return h2 * sg

@@ -1,0 +1,235 @@
+from contextlib import ExitStack
+
+import concourse.mybir as mybir
+
+F32 = mybir.dt.float32
+BF16 = mybir.dt.bfloat16
+I32 = mybir.dt.int32
+U32 = mybir.dt.uint32
+U16 = mybir.dt.uint16
+U8 = mybir.dt.uint8
+FP8X4 = mybir.dt.float8_e4m3fn_x4
+ALU = mybir.AluOpType
+ACT = mybir.ActivationFunctionType
+
+P = 128
+PACK = 4
+T = 2048
+S = 512
+W = 384
+HALF = S // 2
+FLOPS = 2 * 2 * 512 * 512 * 512
+
+
+def tile_picked_pqlayknormehq_none_p_kernel(tc, x_words, x_scales, d_words, d_scales, gn, w1, sl, th, offs, k1, n1, n2, n3, n4, out):
+    nc = tc.nc
+    with ExitStack() as ctx:
+        keep = ctx.enter_context(tc.tile_pool(name="keep", bufs=1))
+        psum = ctx.enter_context(tc.psum_pool(name="psum", bufs=1))
+
+        def sb(name, shape, dtype, tag=None):
+            return keep.tile(shape, dtype, name=name, tag=tag or name, align_bytes=64)
+
+        def load_list(name, src):
+            tile = keep.tile(list(src.shape), U16, name=name)
+            nc.sync.dma_start(tile[:], src)
+            return tile
+
+        d_bytes = sb("d_bytes", [P, T], U8)
+        x_bytes = sb("x_bytes", [P, T], U8)
+        planes = sb("planes", [P, 2 * S], U8)
+        nc.vector.memset(planes[:].bitcast(I32), 0)
+
+        half_t = sb("half_t", [P, 1], F32)
+        nc.vector.memset(half_t[:], 0.5)
+        d_table = sb("d_table", [P, T], I32, tag="big")
+        x_table = sb("x_table", [P, T], I32)
+        k1_t = load_list("k1_t", k1)
+        nc.sync.dma_start(d_bytes[:].bitcast(I32), d_scales[0].bitcast(I32).unsqueeze(1).broadcast_to([16, 8, T // 4]))
+        offs_t = load_list("offs_t", offs)
+        nc.sync.dma_start(x_bytes[:].bitcast(I32), x_scales[0].bitcast(I32).unsqueeze(1).broadcast_to([16, 8, T // 4]))
+        nc.sync.dma_start(d_table[:], d_words[0].rearrange("p n t -> p (n t)").bitcast(I32))
+        n2_t = load_list("n2_t", n2)
+        n1_t = load_list("n1_t", n1)
+        n3_t = load_list("n3_t", n3)
+        nc.sync.dma_start(x_table[:], x_words[0].rearrange("p n t -> p (n t)").bitcast(I32))
+        n4_t = load_list("n4_t", n4)
+
+        gn_t = sb("gn_t", [P, PACK], F32)
+        sl_t = sb("sl_t", [P, PACK], F32)
+        th_t = sb("th_t", [P, PACK], F32)
+        for tile, column in ((gn_t, gn), (sl_t, sl), (th_t, th)):
+            nc.gpsimd.dma_start(tile[:], column[:, 0].rearrange("(p t) -> p t", t=PACK))
+
+        d_bytes_g = sb("d_bytes_g", [P, S], U8)
+        x_bytes_g = sb("x_bytes_g", [P, S], U8)
+        stage = sb("stage", [P, 2 * S], U8)
+        nc.vector.tensor_copy(d_bytes_g[:], d_bytes[:].indirect(k1_t[:]))
+        nc.vector.tensor_copy(x_bytes_g[:], x_bytes[:].indirect(offs_t[:]))
+        nc.vector.tensor_copy(
+            stage[:, S:].rearrange("p (t m) -> p m t", t=PACK), d_bytes_g[:].rearrange("p (m t) -> p m t", t=PACK)
+        )
+        nc.vector.tensor_copy(stage[:, :S].bitcast(I32), x_bytes_g[:].bitcast(I32))
+        for q in range(4):
+            nc.scalar.dma_start(planes[32 * q : 32 * q + 4, :].bitcast(I32), stage[32 * q : 32 * q + 32 : 8, :].bitcast(I32))
+
+        d_codes_g = sb("d_codes_g", [P, S], U32)
+        d_codes = sb("d_codes", [P, S], U32)
+        x_codes = sb("x_codes", [P, S], U32)
+        nc.vector.tensor_copy(d_codes_g[:], d_table[:].bitcast(U32).indirect(k1_t[:]))
+        nc.vector.tensor_copy(
+            d_codes[:].rearrange("p (t m) -> p m t", t=PACK), d_codes_g[:].rearrange("p (m t) -> p m t", t=PACK)
+        )
+        nc.vector.tensor_copy(x_codes[:], x_table[:].bitcast(U32).indirect(offs_t[:]))
+
+        w_raw = sb("w_raw", [P, PACK, S], F32, tag="big")
+        nc.sync.dma_start(w_raw[:], w1.rearrange("(p j) c -> p j c", j=PACK))
+
+        win = [sb("win%d" % m, [P, S + 32], F32) for m in range(PACK)]
+        st = [sb("st%d" % m, [P, S if m == 3 else 2 * S], F32) for m in range(PACK)]
+        for m in range(PACK):
+            nc.gpsimd.memset(win[m][:, S:], 0.0)
+        for m in range(3):
+            nc.gpsimd.memset(st[m][:, S:], 0.0)
+        gain = sb("gain", [P, PACK], F32)
+        bias = sb("bias", [P, PACK], F32)
+        neg_th = sb("neg_th", [P, PACK], F32)
+        nc.gpsimd.tensor_scalar(gain[:], gn_t[:], 0.0625, 0.0, ALU.mult, ALU.add)
+        nc.gpsimd.tensor_scalar(neg_th[:], th_t[:], -1.0, 0.0, ALU.mult, ALU.add)
+        nc.gpsimd.tensor_tensor(bias[:], sl_t[:], neg_th[:], ALU.mult)
+
+        h = []
+        for t in range(PACK):
+            acc = psum.tile([P, S], F32, name="acc_h%d" % t)
+            cols = slice(P * t, P * (t + 1))
+            nc.tensor.matmul_mx(
+                out=acc[:],
+                lhsT=d_codes[:, cols].bitcast(FP8X4),
+                lhsT_scale=planes[:, S + P * t : S + P * (t + 1)],
+                rhs=x_codes[:].bitcast(FP8X4),
+                rhs_scale=planes[:, :S],
+                start=True,
+                stop=True,
+            )
+            ht = sb("h%d" % t, [P, S], F32)
+            nc.scalar.copy(ht[:], acc[:])
+            h.append(ht)
+
+        pa0 = sb("pa0", [P, W], F32)
+        mag0 = sb("mag0", [P, W], F32)
+        root0 = sb("root0", [P, W], F32)
+        nc.vector.tensor_copy(pa0[:], h[0][:].indirect(n2_t[:]))
+        nc.vector.scalar_tensor_tensor(mag0[:], pa0[:], -1.0, pa0[:], ALU.mult, ALU.max)
+        nc.scalar.activation(root0[:], mag0[:], ACT.Abs_reciprocal_sqrt, bias=half_t[:], scale=0.0625)
+
+        def roots(tiles, tag=None):
+            name = "".join(str(t) for t in tiles)
+            pa = sb("pa" + name, [P, len(tiles) * W], F32)
+            mag = sb("mag" + name, [P, len(tiles) * W], F32, tag=tag)
+            root = sb("root" + name, [P, len(tiles) * W], F32)
+            for i, t in enumerate(tiles):
+                nc.scalar.activation(pa[:, W * i : W * (i + 1)], h[t][:].indirect(n2_t[:]), ACT.Copy)
+            nc.scalar.activation(mag[:], pa[:], ACT.Abs)
+            nc.scalar.activation(root[:], mag[:], ACT.Abs_reciprocal_sqrt, bias=half_t[:], scale=0.0625)
+            return [root[:, W * i : W * (i + 1)] for i in range(len(tiles))]
+
+        def put_back(t, root, tag=None):
+            part = sb("part%d" % t, [P, W], F32, tag=tag)
+            nc.vector.tensor_tensor(part[:], h[t][:].indirect(n1_t[:]), root, ALU.mult)
+            nc.vector.tensor_tensor(h[t][:].indirect(n1_t[:]), part[:], root, ALU.mult)
+
+        def put_back_scalar(t, root, tag):
+            recip = sb("recip%d" % t, [P, W], F32, tag=tag)
+            ra = sb("ra%d" % t, [P, W], F32)
+            nc.scalar.activation(recip[:], root, ACT.Square)
+            nc.vector.tensor_tensor(ra[:], h[t][:].indirect(n1_t[:]), recip[:], ALU.mult)
+            nc.scalar.activation(h[t][:].indirect(n1_t[:]), ra[:], ACT.Copy)
+
+        def round_scalar(t):
+            nc.scalar.activation(z_rows[:, t, :], h[t][:], ACT.Copy, scale=gain[:, t : t + 1])
+
+        w_codes = sb("w_codes", [P, S], U32)
+        w_scales = sb("w_scales", [P, S], U8)
+        w_dealt = w_raw[:].rearrange("p j (m t) -> p m t j", t=PACK)
+
+        def quantize_w(u, tag=None):
+            grouped = sb("w_grouped%d" % u, [P, HALF, PACK], BF16, tag=tag)
+            nc.vector.tensor_copy(grouped[:].rearrange("p (t m) j -> p m t j", t=2), w_dealt[:, :, 2 * u : 2 * u + 2, :])
+            cols = slice(HALF * u, HALF * (u + 1))
+            nc.vector.quantize_mx(
+                out=w_codes[:, cols].bitcast(FP8X4), scales=w_scales[:, cols], in_=grouped[:].rearrange("p c j -> p (c j)")
+            )
+
+        (root1,) = roots([1])
+        put_back(0, root0[:])
+        quantize_w(0)
+        root2, root3 = roots([2, 3], "late")
+        put_back(1, root1)
+        put_back_scalar(3, root3, "third")
+        z_rows = sb("z_rows", [P, PACK, S], BF16, tag="late")
+        round_scalar(0)
+        round_scalar(1)
+        put_back(2, root2, "third")
+        round_scalar(3)
+        nc.vector.tensor_scalar(z_rows[:, 2, :], h[2][:], gain[:, 2:3], None, ALU.mult)
+
+        z_grouped = sb("z_grouped", [P, S, PACK], BF16, tag="grouped")
+        z_codes = sb("z_codes", [P, S], U32)
+        z_scales = sb("z_scales", [P, S], U8)
+        split = 352
+        nc.vector.tensor_copy(z_grouped[:, :split, :], z_rows[:, :, :split].rearrange("p j c -> p c j"))
+        nc.scalar.copy(z_grouped[:, split:, :], z_rows[:, :, split:].rearrange("p j c -> p c j"))
+        nc.vector.quantize_mx(out=z_codes[:].bitcast(FP8X4), scales=z_scales[:], in_=z_grouped[:].rearrange("p c j -> p (c j)"))
+        quantize_w(1, "grouped")
+
+        acc2, sg, res = [], [], []
+        for m in range(PACK):
+            acc = psum.tile([P, S], F32, name="acc_o%d" % m)
+            cols = slice(P * m, P * (m + 1))
+            nc.tensor.matmul_mx(
+                out=acc[:],
+                lhsT=w_codes[:, cols].bitcast(FP8X4),
+                lhsT_scale=w_scales[:, cols],
+                rhs=z_codes[:].bitcast(FP8X4),
+                rhs_scale=z_scales[:],
+                start=True,
+                stop=True,
+            )
+            acc2.append(acc)
+            for group, name in ((sg, "sg"), (res, "res")):
+                group.append(sb("%s_%d" % (name, m), [P, S], F32))
+        halves = [(slice(HALF * u, HALF * (u + 1)), slice(16 * u, 16 * (u + 1))) for u in range(2)]
+        out_rows = out.rearrange("(p t) c -> p t c", t=PACK)
+
+        def fetch_and_add(m, h2):
+            nc.vector.tensor_scalar(win[m][:, :S], h2[:], -1.0, None, ALU.mult)
+            nc.vector.tensor_tensor(st[m][:, :S], win[m][:].indirect(n3_t[:]), h2[:], ALU.add)
+
+        def gate(m, cols, entries):
+            nc.scalar.activation(
+                sg[m][:, cols], st[m][:].indirect(n4_t[:, entries]), ACT.Sigmoid, bias=bias[:, m : m + 1], scale=sl_t[:, m : m + 1]
+            )
+
+        def finish(m, cols):
+            nc.vector.tensor_tensor(res[m][:, cols], acc2[m][:, cols], sg[m][:, cols], ALU.mult)
+            nc.sync.dma_start(out_rows[:, m, cols], res[m][:, cols])
+
+        other = sb("other", [P, S], F32)
+        h2 = [None] + [sb("h2_%d" % m, [P, S], F32) for m in range(1, PACK)]
+        nc.scalar.copy(win[0][:, :S], acc2[0][:])
+        nc.scalar.activation(other[:], win[0][:].indirect(n3_t[:]), ACT.Copy)
+        nc.vector.tensor_copy(h2[1][:], acc2[1][:])
+        fetch_and_add(1, h2[1])
+        nc.scalar.copy(h2[2][:], acc2[2][:])
+        nc.scalar.copy(h2[3][:], acc2[3][:])
+        nc.vector.tensor_tensor(st[0][:, :S], acc2[0][:], other[:], ALU.subtract)
+        fetch_and_add(2, h2[2])
+        fetch_and_add(3, h2[3])
+        for m in (1, 0, 2):
+            gate(m, slice(0, S), slice(0, S // 16))
+        for cols, entries in halves:
+            gate(3, cols, entries)
+        for m in (1, 0, 2):
+            finish(m, slice(0, S))
+        for cols, entries in halves:
+            finish(3, cols)

@@ -42,6 +42,8 @@ def tile_picked_pqlayknormehq_none_p_kernel(tc, x_words, x_scales, d_words, d_sc
 
         half_t = sb("half_t", [P, 1], F32)
         nc.vector.memset(half_t[:], 0.5)
+        warm = sb("warm", [P, 2], F32)
+        nc.scalar.activation(warm[:, 0:1], half_t[:], ACT.Abs_reciprocal_sqrt, bias=half_t[:], scale=0.0625)
         d_table = sb("d_table", [P, T], I32, tag="big")
         x_table = sb("x_table", [P, T], I32)
         k1_t = load_list("k1_t", k1)
@@ -180,6 +182,8 @@ def tile_picked_pqlayknormehq_none_p_kernel(tc, x_words, x_scales, d_words, d_sc
         nc.vector.tensor_copy(z_grouped[:, :split, :], z_rows[:, :, :split].rearrange("p j c -> p c j"))
         nc.scalar.copy(z_grouped[:, split:, :], z_rows[:, :, split:].rearrange("p j c -> p c j"))
         nc.vector.quantize_mx(out=z_codes[:].bitcast(FP8X4), scales=z_scales[:], in_=z_grouped[:].rearrange("p c j -> p (c j)"))
+        warm2 = sb("warm2", [P, 1], F32, tag="late")
+        nc.scalar.activation(warm2[:], half_t[:], ACT.Sigmoid, bias=half_t[:], scale=1.0)
         quantize_w(1, "grouped")
 
         acc2, sg, res = [], [], []

@@ -82,17 +82,18 @@ def tile_picked_pqlayknormehq_none_p_kernel(tc, x_words, x_scales, d_words, d_sc
         nc.vector.tensor_copy(
             d_codes[:].rearrange("p (t m) -> p m t", t=PACK), d_codes_g[:].rearrange("p (m t) -> p m t", t=PACK)
         )
-        nc.vector.tensor_copy(x_codes[:], x_table[:].bitcast(U32).indirect(offs_t[:]))
+        for u in range(2):
+            nc.vector.tensor_copy(
+                x_codes[:, HALF * u : HALF * (u + 1)], x_table[:].bitcast(U32).indirect(offs_t[:, 16 * u : 16 * (u + 1)])
+            )
 
         w_raw = sb("w_raw", [P, PACK, S], F32, tag="big")
         nc.sync.dma_start(w_raw[:], w1.rearrange("(p j) c -> p j c", j=PACK))
 
         win = [sb("win%d" % m, [P, S + 32], F32) for m in range(PACK)]
-        st = [sb("st%d" % m, [P, S if m == 3 else 2 * S], F32) for m in range(PACK)]
+        st = [sb("st%d" % m, [P, 2 * S], F32) for m in range(PACK)]
         for m in range(PACK):
-            nc.gpsimd.memset(win[m][:, S:], 0.0)
-        for m in range(3):
-            nc.gpsimd.memset(st[m][:, S:], 0.0)
+            nc.vector.memset(win[m][:, S:], 0.0)
         gain = sb("gain", [P, PACK], F32)
         bias = sb("bias", [P, PACK], F32)
         neg_th = sb("neg_th", [P, PACK], F32)
@@ -100,52 +101,56 @@ def tile_picked_pqlayknormehq_none_p_kernel(tc, x_words, x_scales, d_words, d_sc
         nc.gpsimd.tensor_scalar(neg_th[:], th_t[:], -1.0, 0.0, ALU.mult, ALU.add)
         nc.gpsimd.tensor_tensor(bias[:], sl_t[:], neg_th[:], ALU.mult)
 
-        h = []
-        for t in range(PACK):
-            acc = psum.tile([P, S], F32, name="acc_h%d" % t)
-            cols = slice(P * t, P * (t + 1))
+        acc1 = [psum.tile([P, S], F32, name="acc_h%d" % t) for t in range(PACK)]
+        h = [sb("h%d" % t, [P, S], F32) for t in range(PACK)]
+        passes = [(t, slice(HALF * u, HALF * (u + 1))) for u in range(2) for t in range(2)]
+        passes = passes + [(t, slice(0, S)) for t in range(2, PACK)]
+        for t, cols in passes:
             nc.tensor.matmul_mx(
-                out=acc[:],
-                lhsT=d_codes[:, cols].bitcast(FP8X4),
+                out=acc1[t][:, cols],
+                lhsT=d_codes[:, P * t : P * (t + 1)].bitcast(FP8X4),
                 lhsT_scale=planes[:, S + P * t : S + P * (t + 1)],
-                rhs=x_codes[:].bitcast(FP8X4),
-                rhs_scale=planes[:, :S],
+                rhs=x_codes[:, cols].bitcast(FP8X4),
+                rhs_scale=planes[:, cols],
                 start=True,
                 stop=True,
             )
-            ht = sb("h%d" % t, [P, S], F32)
-            nc.scalar.copy(ht[:], acc[:])
-            h.append(ht)
-
-        pa0 = sb("pa0", [P, W], F32)
-        mag0 = sb("mag0", [P, W], F32)
-        root0 = sb("root0", [P, W], F32)
-        nc.vector.tensor_copy(pa0[:], h[0][:].indirect(n2_t[:]))
-        nc.vector.scalar_tensor_tensor(mag0[:], pa0[:], -1.0, pa0[:], ALU.mult, ALU.max)
-        nc.scalar.activation(root0[:], mag0[:], ACT.Abs_reciprocal_sqrt, bias=half_t[:], scale=0.0625)
+        for t in range(PACK):
+            nc.scalar.copy(h[t][:], acc1[t][:])
 
         def roots(tiles, tag=None):
             name = "".join(str(t) for t in tiles)
             pa = sb("pa" + name, [P, len(tiles) * W], F32)
-            mag = sb("mag" + name, [P, len(tiles) * W], F32, tag=tag)
-            root = sb("root" + name, [P, len(tiles) * W], F32)
-            for i, t in enumerate(tiles):
-                nc.scalar.activation(pa[:, W * i : W * (i + 1)], h[t][:].indirect(n2_t[:]), ACT.Copy)
-            nc.scalar.activation(mag[:], pa[:], ACT.Abs)
+            mag = sb("mag" + name, [P, len(tiles) * W], F32)
+            root = sb("root" + name, [P, len(tiles) * W], F32, tag=tag)
+            if tiles == [0]:
+                nc.vector.tensor_copy(pa[:], h[0][:].indirect(n2_t[:]))
+                nc.vector.scalar_tensor_tensor(mag[:], pa[:], -1.0, pa[:], ALU.mult, ALU.max)
+            else:
+                for i, t in enumerate(tiles):
+                    nc.scalar.activation(pa[:, W * i : W * (i + 1)], h[t][:].indirect(n2_t[:]), ACT.Copy)
+                nc.scalar.activation(mag[:], pa[:], ACT.Abs)
             nc.scalar.activation(root[:], mag[:], ACT.Abs_reciprocal_sqrt, bias=half_t[:], scale=0.0625)
-            return [root[:, W * i : W * (i + 1)] for i in range(len(tiles))]
+            return root
 
-        def put_back(t, root, tag=None):
-            part = sb("part%d" % t, [P, W], F32, tag=tag)
-            nc.vector.tensor_tensor(part[:], h[t][:].indirect(n1_t[:]), root, ALU.mult)
-            nc.vector.tensor_tensor(h[t][:].indirect(n1_t[:]), part[:], root, ALU.mult)
+        def squared(root, name):
+            recip = sb(name, list(root.shape), F32)
+            nc.scalar.activation(recip[:], root[:], ACT.Square)
+            return recip
 
-        def put_back_scalar(t, root, tag):
-            recip = sb("recip%d" % t, [P, W], F32, tag=tag)
-            ra = sb("ra%d" % t, [P, W], F32)
-            nc.scalar.activation(recip[:], root, ACT.Square)
-            nc.vector.tensor_tensor(ra[:], h[t][:].indirect(n1_t[:]), recip[:], ALU.mult)
-            nc.scalar.activation(h[t][:].indirect(n1_t[:]), ra[:], ACT.Copy)
+        def fetch_old(t, factor=None):
+            old = sb("old%d" % t, [P, W], F32, tag={0: "pa0", 3: "last"}.get(t))
+            if factor is None:
+                nc.vector.tensor_copy(old[:], h[t][:].indirect(n1_t[:]))
+            else:
+                nc.vector.tensor_tensor(old[:], h[t][:].indirect(n1_t[:]), factor, ALU.mult)
+            return old
+
+        def put_back(t, old, factor):
+            nc.vector.tensor_tensor(h[t][:].indirect(n1_t[:]), old[:], factor, ALU.mult)
+
+        def round_vector(t):
+            nc.vector.tensor_scalar(z_rows[:, t, :], h[t][:], gain[:, t : t + 1], None, ALU.mult)
 
         def round_scalar(t):
             nc.scalar.activation(z_rows[:, t, :], h[t][:], ACT.Copy, scale=gain[:, t : t + 1])
@@ -154,60 +159,67 @@ def tile_picked_pqlayknormehq_none_p_kernel(tc, x_words, x_scales, d_words, d_sc
         w_scales = sb("w_scales", [P, S], U8)
         w_dealt = w_raw[:].rearrange("p j (m t) -> p m t j", t=PACK)
 
-        def quantize_w(u, tag=None):
+        def quantize_w(u, copy, tag=None):
             grouped = sb("w_grouped%d" % u, [P, HALF, PACK], BF16, tag=tag)
-            nc.vector.tensor_copy(grouped[:].rearrange("p (t m) j -> p m t j", t=2), w_dealt[:, :, 2 * u : 2 * u + 2, :])
+            copy(grouped[:].rearrange("p (t m) j -> p m t j", t=2), w_dealt[:, :, 2 * u : 2 * u + 2, :])
             cols = slice(HALF * u, HALF * (u + 1))
             nc.vector.quantize_mx(
                 out=w_codes[:, cols].bitcast(FP8X4), scales=w_scales[:, cols], in_=grouped[:].rearrange("p c j -> p (c j)")
             )
 
-        (root1,) = roots([1])
-        put_back(0, root0[:])
-        quantize_w(0)
-        root2, root3 = roots([2, 3], "late")
-        put_back(1, root1)
-        put_back_scalar(3, root3, "third")
+        recip0 = squared(roots([0]), "recip0")
+        old0 = fetch_old(0)
+        root1 = roots([1])
+        recip23 = squared(roots([2, 3], "late"), "recip23")
+        put_back(0, old0, recip0[:])
+        put_back(1, fetch_old(1, root1[:]), root1[:])
+        ra3 = fetch_old(3, recip23[:, W:])
+        put_back(2, fetch_old(2), recip23[:, :W])
+        quantize_w(0, nc.vector.tensor_copy)
         z_rows = sb("z_rows", [P, PACK, S], BF16, tag="late")
         round_scalar(0)
         round_scalar(1)
-        put_back(2, root2, "third")
-        round_scalar(3)
-        nc.vector.tensor_scalar(z_rows[:, 2, :], h[2][:], gain[:, 2:3], None, ALU.mult)
+        nc.scalar.activation(h[3][:].indirect(n1_t[:]), ra3[:], ACT.Copy)
+        round_vector(2)
+        round_vector(3)
 
-        z_grouped = sb("z_grouped", [P, S, PACK], BF16, tag="grouped")
+        z_grouped = sb("z_grouped", [P, S, PACK], BF16)
         z_codes = sb("z_codes", [P, S], U32)
         z_scales = sb("z_scales", [P, S], U8)
-        split = 352
-        nc.vector.tensor_copy(z_grouped[:, :split, :], z_rows[:, :, :split].rearrange("p j c -> p c j"))
-        nc.scalar.copy(z_grouped[:, split:, :], z_rows[:, :, split:].rearrange("p j c -> p c j"))
-        nc.vector.quantize_mx(out=z_codes[:].bitcast(FP8X4), scales=z_scales[:], in_=z_grouped[:].rearrange("p c j -> p (c j)"))
-        warm2 = sb("warm2", [P, 1], F32, tag="late")
+        for cols in (slice(0, HALF), slice(HALF, S)):
+            nc.vector.tensor_copy(
+                z_grouped[:, cols, :].rearrange("p (c i) j -> p c j i", i=4), z_rows[:, :, cols].rearrange("p j (c i) -> p c j i", i=4)
+            )
+        for cols in (slice(0, HALF), slice(HALF, S)):
+            nc.vector.quantize_mx(
+                out=z_codes[:, cols].bitcast(FP8X4), scales=z_scales[:, cols], in_=z_grouped[:, cols, :].rearrange("p c j -> p (c j)")
+            )
+        warm2 = sb("warm2", [P, 1], F32, tag="last")
         nc.scalar.activation(warm2[:], half_t[:], ACT.Sigmoid, bias=half_t[:], scale=1.0)
-        quantize_w(1, "grouped")
+        quantize_w(1, nc.scalar.copy, "last")
 
-        acc2, sg, res = [], [], []
-        for m in range(PACK):
-            acc = psum.tile([P, S], F32, name="acc_o%d" % m)
-            cols = slice(P * m, P * (m + 1))
+        acc2 = [psum.tile([P, S], F32, name="acc_o%d" % m) for m in range(PACK)]
+        sg = [sb("sg%d" % m, [P, S], F32) for m in range(PACK)]
+        res = [sb("res%d" % m, [P, S], F32) for m in range(PACK)]
+        passes = [(m, slice(HALF * u, HALF * (u + 1))) for u in range(2) for m in range(2)]
+        passes = passes + [(m, slice(0, S)) for m in range(2, PACK)]
+        for m, cols in passes:
+            rows = slice(P * m, P * (m + 1))
             nc.tensor.matmul_mx(
-                out=acc[:],
-                lhsT=w_codes[:, cols].bitcast(FP8X4),
-                lhsT_scale=w_scales[:, cols],
-                rhs=z_codes[:].bitcast(FP8X4),
-                rhs_scale=z_scales[:],
+                out=acc2[m][:, cols],
+                lhsT=w_codes[:, rows].bitcast(FP8X4),
+                lhsT_scale=w_scales[:, rows],
+                rhs=z_codes[:, cols].bitcast(FP8X4),
+                rhs_scale=z_scales[:, cols],
                 start=True,
                 stop=True,
             )
-            acc2.append(acc)
-            for group, name in ((sg, "sg"), (res, "res")):
-                group.append(sb("%s_%d" % (name, m), [P, S], F32))
         halves = [(slice(HALF * u, HALF * (u + 1)), slice(16 * u, 16 * (u + 1))) for u in range(2)]
         out_rows = out.rearrange("(p t) c -> p t c", t=PACK)
 
         def fetch_and_add(m, h2):
-            nc.vector.tensor_scalar(win[m][:, :S], h2[:], -1.0, None, ALU.mult)
-            nc.vector.tensor_tensor(st[m][:, :S], win[m][:].indirect(n3_t[:]), h2[:], ALU.add)
+            nc.vector.tensor_scalar(win[m][:, :S], h2, -1.0, None, ALU.mult)
+            nc.vector.tensor_tensor(st[m][:, :S], win[m][:].indirect(n3_t[:]), h2, ALU.add)
 
         def gate(m, cols, entries):
             nc.scalar.activation(
@@ -218,22 +230,22 @@ def tile_picked_pqlayknormehq_none_p_kernel(tc, x_words, x_scales, d_words, d_sc
             nc.vector.tensor_tensor(res[m][:, cols], acc2[m][:, cols], sg[m][:, cols], ALU.mult)
             nc.sync.dma_start(out_rows[:, m, cols], res[m][:, cols])
 
-        other = sb("other", [P, S], F32)
-        h2 = [None] + [sb("h2_%d" % m, [P, S], F32) for m in range(1, PACK)]
-        nc.scalar.copy(win[0][:, :S], acc2[0][:])
-        nc.scalar.activation(other[:], win[0][:].indirect(n3_t[:]), ACT.Copy)
-        nc.vector.tensor_copy(h2[1][:], acc2[1][:])
-        fetch_and_add(1, h2[1])
-        nc.scalar.copy(h2[2][:], acc2[2][:])
-        nc.scalar.copy(h2[3][:], acc2[3][:])
-        nc.vector.tensor_tensor(st[0][:, :S], acc2[0][:], other[:], ALU.subtract)
+        other = st[1][:, S:]
+        h2 = [st[m][:, S:] for m in range(PACK)]
+        nc.vector.tensor_copy(h2[0], acc2[0][:])
+        fetch_and_add(0, h2[0])
+        nc.scalar.copy(win[1][:, :S], acc2[1][:])
+        nc.scalar.activation(other, win[1][:].indirect(n3_t[:]), ACT.Copy)
+        nc.scalar.copy(h2[2], acc2[2][:])
+        nc.scalar.copy(h2[3], acc2[3][:])
+        nc.vector.tensor_tensor(st[1][:, :S], acc2[1][:], other, ALU.subtract)
         fetch_and_add(2, h2[2])
         fetch_and_add(3, h2[3])
-        for m in (1, 0, 2):
+        for m in range(3):
             gate(m, slice(0, S), slice(0, S // 16))
         for cols, entries in halves:
             gate(3, cols, entries)
-        for m in (1, 0, 2):
+        for m in range(3):
             finish(m, slice(0, S))
         for cols, entries in halves:
             finish(3, cols)

@@ -44,8 +44,8 @@ def tile_picked_pqlayknormehq_none_p_kernel(tc, x_words, x_scales, d_words, d_sc
         nc.vector.memset(half_t[:], 0.5)
         warm = sb("warm", [P, 2], F32)
         nc.scalar.activation(warm[:, 0:1], half_t[:], ACT.Abs_reciprocal_sqrt, bias=half_t[:], scale=0.0625)
-        d_table = sb("d_table", [P, T], I32, tag="big")
-        x_table = sb("x_table", [P, T], I32)
+        d_table = sb("d_table", [P, T], I32)
+        x_table = sb("x_table", [P, T], I32, tag="big")
         k1_t = load_list("k1_t", k1)
         nc.sync.dma_start(d_bytes[:].bitcast(I32), d_scales[0].bitcast(I32).unsqueeze(1).broadcast_to([16, 8, T // 4]))
         offs_t = load_list("offs_t", offs)
@@ -56,12 +56,6 @@ def tile_picked_pqlayknormehq_none_p_kernel(tc, x_words, x_scales, d_words, d_sc
         n3_t = load_list("n3_t", n3)
         nc.sync.dma_start(x_table[:], x_words[0].rearrange("p n t -> p (n t)").bitcast(I32))
         n4_t = load_list("n4_t", n4)
-
-        gn_t = sb("gn_t", [P, PACK], F32)
-        sl_t = sb("sl_t", [P, PACK], F32)
-        th_t = sb("th_t", [P, PACK], F32)
-        for tile, column in ((gn_t, gn), (sl_t, sl), (th_t, th)):
-            nc.gpsimd.dma_start(tile[:], column[:, 0].rearrange("(p t) -> p t", t=PACK))
 
         d_bytes_g = sb("d_bytes_g", [P, S], U8)
         x_bytes_g = sb("x_bytes_g", [P, S], U8)
@@ -87,6 +81,10 @@ def tile_picked_pqlayknormehq_none_p_kernel(tc, x_words, x_scales, d_words, d_sc
                 x_codes[:, HALF * u : HALF * (u + 1)], x_table[:].bitcast(U32).indirect(offs_t[:, 16 * u : 16 * (u + 1)])
             )
 
+        columns = sb("columns", [P, 3, 2 * PACK], F32, tag="stage")
+        gn_t, sl_t, th_t = (columns[:, i, :PACK] for i in range(3))
+        for tile, column in ((gn_t, gn), (sl_t, sl), (th_t, th)):
+            nc.sync.dma_start(tile, column[:, 0].rearrange("(p t) -> p t", t=PACK))
         w_raw = sb("w_raw", [P, PACK, S], F32, tag="big")
         nc.sync.dma_start(w_raw[:], w1.rearrange("(p j) c -> p j c", j=PACK))
 
@@ -94,20 +92,9 @@ def tile_picked_pqlayknormehq_none_p_kernel(tc, x_words, x_scales, d_words, d_sc
         st = [sb("st%d" % m, [P, 2 * S], F32) for m in range(PACK)]
         for m in range(PACK):
             nc.vector.memset(win[m][:, S:], 0.0)
-        gain = sb("gain", [P, PACK], F32)
-        bias = sb("bias", [P, PACK], F32)
-        neg_th = sb("neg_th", [P, PACK], F32)
-        nc.gpsimd.tensor_scalar(gain[:], gn_t[:], 0.0625, 0.0, ALU.mult, ALU.add)
-        nc.gpsimd.tensor_scalar(neg_th[:], th_t[:], -1.0, 0.0, ALU.mult, ALU.add)
-        nc.gpsimd.tensor_tensor(bias[:], sl_t[:], neg_th[:], ALU.mult)
-
-        acc1 = [psum.tile([P, S], F32, name="acc_h%d" % t) for t in range(PACK)]
-        h = [sb("h%d" % t, [P, S], F32) for t in range(PACK)]
-        passes = [(t, slice(HALF * u, HALF * (u + 1))) for u in range(2) for t in range(2)]
-        passes = passes + [(t, slice(0, S)) for t in range(2, PACK)]
-        for t, cols in passes:
+        def first_product(t, cols, acc):
             nc.tensor.matmul_mx(
-                out=acc1[t][:, cols],
+                out=acc[:],
                 lhsT=d_codes[:, P * t : P * (t + 1)].bitcast(FP8X4),
                 lhsT_scale=planes[:, S + P * t : S + P * (t + 1)],
                 rhs=x_codes[:, cols].bitcast(FP8X4),
@@ -115,8 +102,15 @@ def tile_picked_pqlayknormehq_none_p_kernel(tc, x_words, x_scales, d_words, d_sc
                 start=True,
                 stop=True,
             )
-        for t in range(PACK):
-            nc.scalar.copy(h[t][:], acc1[t][:])
+            nc.scalar.copy(h[t][:, cols], acc[:])
+
+        h = [sb("h%d" % t, [P, S], F32) for t in range(PACK)]
+        for u in range(2):
+            for t in range(2):
+                acc = psum.tile([P, HALF], F32, name="acc_h%d_%d" % (t, u), tag="bank%d" % (t + PACK * (1 - u)))
+                first_product(t, slice(HALF * u, HALF * (u + 1)), acc)
+        for t in range(2, PACK):
+            first_product(t, slice(0, S), psum.tile([P, S], F32, name="acc_h%d" % t, tag="bank%d" % t))
 
         def roots(tiles, tag=None):
             name = "".join(str(t) for t in tiles)
@@ -169,6 +163,10 @@ def tile_picked_pqlayknormehq_none_p_kernel(tc, x_words, x_scales, d_words, d_sc
 
         recip0 = squared(roots([0]), "recip0")
         old0 = fetch_old(0)
+        gain = sb("gain", [P, PACK], F32, tag="root0")
+        bias = sb("bias", [P, PACK], F32, tag="mag0")
+        nc.vector.tensor_scalar(gain[:], gn_t, 0.0625, None, ALU.mult)
+        nc.vector.scalar_tensor_tensor(bias[:], sl_t, -1.0, th_t, ALU.mult, ALU.mult)
         root1 = roots([1])
         recip23 = squared(roots([2, 3], "late"), "recip23")
         put_back(0, old0, recip0[:])
@@ -198,7 +196,7 @@ def tile_picked_pqlayknormehq_none_p_kernel(tc, x_words, x_scales, d_words, d_sc
         nc.scalar.activation(warm2[:], half_t[:], ACT.Sigmoid, bias=half_t[:], scale=1.0)
         quantize_w(1, nc.scalar.copy, "last")
 
-        acc2 = [psum.tile([P, S], F32, name="acc_o%d" % m) for m in range(PACK)]
+        acc2 = [psum.tile([P, S], F32, name="acc_o%d" % m, tag="bank%d" % (PACK + m)) for m in range(PACK)]
         sg = [sb("sg%d" % m, [P, S], F32) for m in range(PACK)]
         res = [sb("res%d" % m, [P, S], F32) for m in range(PACK)]
         passes = [(m, slice(HALF * u, HALF * (u + 1))) for u in range(2) for m in range(2)]

@@ -14,236 +14,265 @@ ACT = mybir.ActivationFunctionType
 
 P = 128
 PACK = 4
-T = 2048
+QUADRANT = 32
+BLOCK_PARTITIONS = 8
+PLANE_START = 4
+TABLE = 2048
 S = 512
-W = 384
 HALF = S // 2
-FLOPS = 2 * 2 * 512 * 512 * 512
+W = 384
+PER_COLUMN = 16
+SPARE = 32
+SIXTEENTH = 0.0625
+FLOPS = 2 * 2 * S * S * S
 
 
-def tile_picked_pqlayknormehq_none_p_kernel(tc, x_words, x_scales, d_words, d_scales, gn, w1, sl, th, offs, k1, n1, n2, n3, n4, out):
+def tile_picked_pqlayknormehq_none_p_kernel(
+    tc, x_words, x_scales, d_words, d_scales, gn, w1, sl, th, offs, k1, n1, n2, n3, n4, out
+):
     nc = tc.nc
+    halves = [slice(0, HALF), slice(HALF, S)]
+
     with ExitStack() as ctx:
         keep = ctx.enter_context(tc.tile_pool(name="keep", bufs=1))
         psum = ctx.enter_context(tc.psum_pool(name="psum", bufs=1))
 
-        def sb(name, shape, dtype, tag=None):
+        def sbuf(name, shape, dtype, tag=None):
             return keep.tile(shape, dtype, name=name, tag=tag or name, align_bytes=64)
 
-        def load_list(name, src):
-            tile = keep.tile(list(src.shape), U16, name=name)
-            nc.sync.dma_start(tile[:], src)
+        def load_list(name, source):
+            tile = keep.tile(list(source.shape), U16, name=name)
+            nc.sync.dma_start(tile[:], source)
             return tile
 
-        d_bytes = sb("d_bytes", [P, T], U8)
-        x_bytes = sb("x_bytes", [P, T], U8)
-        planes = sb("planes", [P, 2 * S], U8)
-        nc.vector.memset(planes[:].bitcast(I32), 0)
+        def load_scale_rows(tile, scales):
+            rows = scales[0].bitcast(I32).unsqueeze(1)
+            nc.sync.dma_start(tile[:].bitcast(I32), rows.broadcast_to([P // BLOCK_PARTITIONS, BLOCK_PARTITIONS, TABLE // 4]))
 
-        half_t = sb("half_t", [P, 1], F32)
-        nc.vector.memset(half_t[:], 0.5)
-        warm = sb("warm", [P, 2], F32)
-        nc.scalar.activation(warm[:, 0:1], half_t[:], ACT.Abs_reciprocal_sqrt, bias=half_t[:], scale=0.0625)
-        d_table = sb("d_table", [P, T], I32)
-        x_table = sb("x_table", [P, T], I32, tag="big")
-        k1_t = load_list("k1_t", k1)
-        nc.sync.dma_start(d_bytes[:].bitcast(I32), d_scales[0].bitcast(I32).unsqueeze(1).broadcast_to([16, 8, T // 4]))
-        offs_t = load_list("offs_t", offs)
-        nc.sync.dma_start(x_bytes[:].bitcast(I32), x_scales[0].bitcast(I32).unsqueeze(1).broadcast_to([16, 8, T // 4]))
-        nc.sync.dma_start(d_table[:], d_words[0].rearrange("p n t -> p (n t)").bitcast(I32))
-        n2_t = load_list("n2_t", n2)
-        n1_t = load_list("n1_t", n1)
-        n3_t = load_list("n3_t", n3)
-        nc.sync.dma_start(x_table[:], x_words[0].rearrange("p n t -> p (n t)").bitcast(I32))
-        n4_t = load_list("n4_t", n4)
+        def load_words(tile, words):
+            nc.sync.dma_start(tile[:], words[0].rearrange("p n t -> p (n t)").bitcast(I32))
 
-        d_bytes_g = sb("d_bytes_g", [P, S], U8)
-        x_bytes_g = sb("x_bytes_g", [P, S], U8)
-        stage = sb("stage", [P, 2 * S], U8)
-        nc.vector.tensor_copy(d_bytes_g[:], d_bytes[:].indirect(k1_t[:]))
-        nc.vector.tensor_copy(x_bytes_g[:], x_bytes[:].indirect(offs_t[:]))
-        nc.vector.tensor_copy(
-            stage[:, S:].rearrange("p (t m) -> p m t", t=PACK), d_bytes_g[:].rearrange("p (m t) -> p m t", t=PACK)
-        )
-        nc.vector.tensor_copy(stage[:, :S].bitcast(I32), x_bytes_g[:].bitcast(I32))
-        for q in range(4):
-            nc.scalar.dma_start(planes[32 * q : 32 * q + 4, :].bitcast(I32), stage[32 * q : 32 * q + 32 : 8, :].bitcast(I32))
+        def entries(cols):
+            return slice(cols.start // PER_COLUMN, cols.stop // PER_COLUMN)
 
-        d_codes_g = sb("d_codes_g", [P, S], U32)
-        d_codes = sb("d_codes", [P, S], U32)
-        x_codes = sb("x_codes", [P, S], U32)
-        nc.vector.tensor_copy(d_codes_g[:], d_table[:].bitcast(U32).indirect(k1_t[:]))
-        nc.vector.tensor_copy(
-            d_codes[:].rearrange("p (t m) -> p m t", t=PACK), d_codes_g[:].rearrange("p (m t) -> p m t", t=PACK)
-        )
-        for u in range(2):
+        def deal(target, source):
             nc.vector.tensor_copy(
-                x_codes[:, HALF * u : HALF * (u + 1)], x_table[:].bitcast(U32).indirect(offs_t[:, 16 * u : 16 * (u + 1)])
+                target.rearrange("p (t m) -> p m t", t=PACK), source.rearrange("p (m t) -> p m t", t=PACK)
             )
 
-        columns = sb("columns", [P, 3, 2 * PACK], F32, tag="stage")
-        gn_t, sl_t, th_t = (columns[:, i, :PACK] for i in range(3))
-        for tile, column in ((gn_t, gn), (sl_t, sl), (th_t, th)):
-            nc.sync.dma_start(tile, column[:, 0].rearrange("(p t) -> p t", t=PACK))
-        w_raw = sb("w_raw", [P, PACK, S], F32, tag="big")
+        half_bias = sbuf("half_bias", [P, 1], F32)
+        nc.vector.memset(half_bias[:], 0.5)
+        warm_root = sbuf("warm_root", [P, 1], F32)
+        nc.scalar.activation(warm_root[:], half_bias[:], ACT.Abs_reciprocal_sqrt, bias=half_bias[:], scale=SIXTEENTH)
+
+        d_scale_table = sbuf("d_scale_table", [P, TABLE], U8)
+        x_scale_table = sbuf("x_scale_table", [P, TABLE], U8)
+        d_word_table = sbuf("d_word_table", [P, TABLE], I32)
+        x_word_table = sbuf("x_word_table", [P, TABLE], I32)
+        k1_list = load_list("k1_list", k1)
+        load_scale_rows(d_scale_table, d_scales)
+        offs_list = load_list("offs_list", offs)
+        load_scale_rows(x_scale_table, x_scales)
+        load_words(d_word_table, d_words)
+        n2_list = load_list("n2_list", n2)
+        n1_list = load_list("n1_list", n1)
+        n3_list = load_list("n3_list", n3)
+        load_words(x_word_table, x_words)
+        n4_list = load_list("n4_list", n4)
+
+        d_scale_picked = sbuf("d_scale_picked", [P, S], U8)
+        x_scale_picked = sbuf("x_scale_picked", [P, S], U8)
+        planes = sbuf("planes", [P, 2 * S], U8)
+        nc.vector.tensor_copy(d_scale_picked[:], d_scale_table[:].indirect(k1_list[:]))
+        nc.vector.tensor_copy(x_scale_picked[:], x_scale_table[:].indirect(offs_list[:]))
+        deal(planes[:, S:], d_scale_picked[:])
+        nc.vector.tensor_copy(planes[:, :S].bitcast(I32), x_scale_picked[:].bitcast(I32))
+        for i in range(1, QUADRANT // BLOCK_PARTITIONS):
+            nc.scalar.dma_start(
+                planes[PLANE_START + i : P : QUADRANT, :].bitcast(I32),
+                planes[BLOCK_PARTITIONS * i : P : QUADRANT, :].bitcast(I32),
+            )
+
+        d_word_picked = sbuf("d_word_picked", [P, S], U32)
+        d_codes = sbuf("d_codes", [P, S], U32)
+        x_codes = sbuf("x_codes", [P, S], U32)
+        nc.vector.tensor_copy(d_word_picked[:], d_word_table[:].bitcast(U32).indirect(k1_list[:]))
+        deal(d_codes[:], d_word_picked[:])
+        for cols in halves:
+            nc.vector.tensor_copy(x_codes[:, cols], x_word_table[:].bitcast(U32).indirect(offs_list[:, entries(cols)]))
+
+        vectors = sbuf("vectors", [P, 3, 2 * PACK], F32, tag="d_word_picked")
+        gn_col, sl_col, th_col = (vectors[:, i, :PACK] for i in range(3))
+        for target, source in ((gn_col, gn), (sl_col, sl), (th_col, th)):
+            nc.sync.dma_start(target, source[:, 0].rearrange("(p t) -> p t", t=PACK))
+        w_raw = sbuf("w_raw", [P, PACK, S], F32, tag="x_word_table")
         nc.sync.dma_start(w_raw[:], w1.rearrange("(p j) c -> p j c", j=PACK))
 
-        win = [sb("win%d" % m, [P, S + 32], F32) for m in range(PACK)]
-        st = [sb("st%d" % m, [P, 2 * S], F32) for m in range(PACK)]
+        last = PACK - 1
+        n3_window = [sbuf("n3_window%d" % m, [P, S + SPARE], F32) for m in range(PACK)]
+        st = [sbuf("st%d" % m, [P, S if m == last else 2 * S], F32) for m in range(PACK)]
         for m in range(PACK):
-            nc.vector.memset(win[m][:, S:], 0.0)
-        def first_product(t, cols, acc):
+            nc.vector.memset(n3_window[m][:, S:], 0.0)
+
+        h = [sbuf("h%d" % t, [P, S], F32) for t in range(PACK)]
+
+        def first_product(t, cols, bank):
+            acc = psum.tile([P, cols.stop - cols.start], F32, name="acc_h%d_%d" % (t, bank), tag="bank%d" % bank)
             nc.tensor.matmul_mx(
                 out=acc[:],
                 lhsT=d_codes[:, P * t : P * (t + 1)].bitcast(FP8X4),
-                lhsT_scale=planes[:, S + P * t : S + P * (t + 1)],
+                lhsT_scale=planes[PLANE_START:, S + P * t : S + P * (t + 1)],
                 rhs=x_codes[:, cols].bitcast(FP8X4),
-                rhs_scale=planes[:, cols],
+                rhs_scale=planes[PLANE_START:, cols],
                 start=True,
                 stop=True,
             )
             nc.scalar.copy(h[t][:, cols], acc[:])
 
-        h = [sb("h%d" % t, [P, S], F32) for t in range(PACK)]
-        for u in range(2):
-            for t in range(2):
-                acc = psum.tile([P, HALF], F32, name="acc_h%d_%d" % (t, u), tag="bank%d" % (t + PACK * (1 - u)))
-                first_product(t, slice(HALF * u, HALF * (u + 1)), acc)
+        for t in range(2):
+            first_product(t, halves[0], PACK + t)
+        for t in range(2):
+            first_product(t, halves[1], t)
         for t in range(2, PACK):
-            first_product(t, slice(0, S), psum.tile([P, S], F32, name="acc_h%d" % t, tag="bank%d" % t))
+            first_product(t, slice(0, S), t)
 
-        def roots(tiles, tag=None):
-            name = "".join(str(t) for t in tiles)
-            pa = sb("pa" + name, [P, len(tiles) * W], F32)
-            mag = sb("mag" + name, [P, len(tiles) * W], F32)
-            root = sb("root" + name, [P, len(tiles) * W], F32, tag=tag)
-            if tiles == [0]:
-                nc.vector.tensor_copy(pa[:], h[0][:].indirect(n2_t[:]))
-                nc.vector.scalar_tensor_tensor(mag[:], pa[:], -1.0, pa[:], ALU.mult, ALU.max)
-            else:
-                for i, t in enumerate(tiles):
-                    nc.scalar.activation(pa[:, W * i : W * (i + 1)], h[t][:].indirect(n2_t[:]), ACT.Copy)
-                nc.scalar.activation(mag[:], pa[:], ACT.Abs)
-            nc.scalar.activation(root[:], mag[:], ACT.Abs_reciprocal_sqrt, bias=half_t[:], scale=0.0625)
+        def inverse_root(magnitude, name):
+            root = sbuf(name, list(magnitude.shape), F32)
+            nc.scalar.activation(root[:], magnitude[:], ACT.Abs_reciprocal_sqrt, bias=half_bias[:], scale=SIXTEENTH)
             return root
 
-        def squared(root, name):
-            recip = sb(name, list(root.shape), F32)
-            nc.scalar.activation(recip[:], root[:], ACT.Square)
-            return recip
+        def magnitude_on_scalar(tiles, name):
+            pa = sbuf("pa" + name, [P, len(tiles) * W], F32)
+            magnitude = sbuf("magnitude" + name, [P, len(tiles) * W], F32)
+            for i, t in enumerate(tiles):
+                nc.scalar.activation(pa[:, W * i : W * (i + 1)], h[t][:].indirect(n2_list[:]), ACT.Copy)
+            nc.scalar.activation(magnitude[:], pa[:], ACT.Abs)
+            return magnitude
 
-        def fetch_old(t, factor=None):
-            old = sb("old%d" % t, [P, W], F32, tag={0: "pa0", 3: "last"}.get(t))
-            if factor is None:
-                nc.vector.tensor_copy(old[:], h[t][:].indirect(n1_t[:]))
-            else:
-                nc.vector.tensor_tensor(old[:], h[t][:].indirect(n1_t[:]), factor, ALU.mult)
+        def squared(root, name):
+            square = sbuf(name, list(root.shape), F32)
+            nc.scalar.activation(square[:], root[:], ACT.Square)
+            return square
+
+        def fetch_old(t, tag=None):
+            old = sbuf("old%d" % t, [P, W], F32, tag=tag)
+            nc.vector.tensor_copy(old[:], h[t][:].indirect(n1_list[:]))
             return old
 
-        def put_back(t, old, factor):
-            nc.vector.tensor_tensor(h[t][:].indirect(n1_t[:]), old[:], factor, ALU.mult)
+        def fetch_old_times(t, factor):
+            product = sbuf("old_times%d" % t, [P, W], F32)
+            nc.vector.tensor_tensor(product[:], h[t][:].indirect(n1_list[:]), factor, ALU.mult)
+            return product
 
-        def round_vector(t):
-            nc.vector.tensor_scalar(z_rows[:, t, :], h[t][:], gain[:, t : t + 1], None, ALU.mult)
+        def put_back(t, values, factor):
+            nc.vector.tensor_tensor(h[t][:].indirect(n1_list[:]), values[:], factor, ALU.mult)
 
-        def round_scalar(t):
-            nc.scalar.activation(z_rows[:, t, :], h[t][:], ACT.Copy, scale=gain[:, t : t + 1])
-
-        w_codes = sb("w_codes", [P, S], U32)
-        w_scales = sb("w_scales", [P, S], U8)
-        w_dealt = w_raw[:].rearrange("p j (m t) -> p m t j", t=PACK)
+        w_codes = sbuf("w_codes", [P, S], U32)
+        w_plane = sbuf("w_plane", [P, S], U8)
+        w_dealt = w_raw[:].rearrange("p j (m t) -> p m j t", t=PACK)
 
         def quantize_w(u, copy, tag=None):
-            grouped = sb("w_grouped%d" % u, [P, HALF, PACK], BF16, tag=tag)
-            copy(grouped[:].rearrange("p (t m) j -> p m t j", t=2), w_dealt[:, :, 2 * u : 2 * u + 2, :])
-            cols = slice(HALF * u, HALF * (u + 1))
+            grouped = sbuf("w_grouped%d" % u, [P, HALF, PACK], BF16, tag=tag)
+            copy(grouped[:].rearrange("p (t m) j -> p m j t", t=2), w_dealt[:, :, :, 2 * u : 2 * u + 2])
             nc.vector.quantize_mx(
-                out=w_codes[:, cols].bitcast(FP8X4), scales=w_scales[:, cols], in_=grouped[:].rearrange("p c j -> p (c j)")
+                out=w_codes[:, halves[u]].bitcast(FP8X4),
+                scales=w_plane[:, halves[u]],
+                in_=grouped[:].rearrange("p c j -> p (c j)"),
             )
 
-        recip0 = squared(roots([0]), "recip0")
-        old0 = fetch_old(0)
-        gain = sb("gain", [P, PACK], F32, tag="root0")
-        bias = sb("bias", [P, PACK], F32, tag="mag0")
-        nc.vector.tensor_scalar(gain[:], gn_t, 0.0625, None, ALU.mult)
-        nc.vector.scalar_tensor_tensor(bias[:], sl_t, -1.0, th_t, ALU.mult, ALU.mult)
-        root1 = roots([1])
-        recip23 = squared(roots([2, 3], "late"), "recip23")
-        put_back(0, old0, recip0[:])
-        put_back(1, fetch_old(1, root1[:]), root1[:])
-        ra3 = fetch_old(3, recip23[:, W:])
-        put_back(2, fetch_old(2), recip23[:, :W])
+        pa0 = sbuf("pa0", [P, W], F32)
+        magnitude0 = sbuf("magnitude0", [P, W], F32)
+        nc.vector.tensor_copy(pa0[:], h[0][:].indirect(n2_list[:]))
+        nc.vector.scalar_tensor_tensor(magnitude0[:], pa0[:], -1.0, pa0[:], ALU.mult, ALU.max)
+        reciprocal0 = squared(inverse_root(magnitude0, "root0"), "reciprocal0")
+        old0 = fetch_old(0, tag="pa0")
+        gain = sbuf("gain", [P, PACK], F32, tag="root0")
+        bias = sbuf("bias", [P, PACK], F32, tag="magnitude0")
+        nc.vector.tensor_scalar(gain[:], gn_col, SIXTEENTH, None, ALU.mult)
+        nc.vector.scalar_tensor_tensor(bias[:], sl_col, -1.0, th_col, ALU.mult, ALU.mult)
+        root1 = inverse_root(magnitude_on_scalar([1], "1"), "root1")
+        reciprocal23 = squared(inverse_root(magnitude_on_scalar([2, 3], "23"), "root23"), "reciprocal23")
+        put_back(0, old0, reciprocal0[:])
+        put_back(1, fetch_old_times(1, root1[:]), root1[:])
+        ra3 = fetch_old_times(3, reciprocal23[:, W:])
+        put_back(2, fetch_old(2), reciprocal23[:, :W])
         quantize_w(0, nc.vector.tensor_copy)
-        z_rows = sb("z_rows", [P, PACK, S], BF16, tag="late")
-        round_scalar(0)
-        round_scalar(1)
-        nc.scalar.activation(h[3][:].indirect(n1_t[:]), ra3[:], ACT.Copy)
-        round_vector(2)
-        round_vector(3)
 
-        z_grouped = sb("z_grouped", [P, S, PACK], BF16)
-        z_codes = sb("z_codes", [P, S], U32)
-        z_scales = sb("z_scales", [P, S], U8)
-        for cols in (slice(0, HALF), slice(HALF, S)):
+        z_rows = sbuf("z_rows", [P, PACK, S], BF16, tag="root23")
+        for t in range(2):
+            nc.scalar.activation(z_rows[:, t, :], h[t][:], ACT.Copy, scale=gain[:, t : t + 1])
+        nc.scalar.activation(h[3][:].indirect(n1_list[:]), ra3[:], ACT.Copy)
+        for t in range(2, PACK):
+            nc.vector.tensor_scalar(z_rows[:, t, :], h[t][:], gain[:, t : t + 1], None, ALU.mult)
+
+        z_grouped = sbuf("z_grouped", [P, S, PACK], BF16)
+        z_codes = sbuf("z_codes", [P, S], U32)
+        z_plane = sbuf("z_plane", [P, S], U8)
+        for cols in halves:
             nc.vector.tensor_copy(
-                z_grouped[:, cols, :].rearrange("p (c i) j -> p c j i", i=4), z_rows[:, :, cols].rearrange("p j (c i) -> p c j i", i=4)
+                z_grouped[:, cols, :].rearrange("p (c i) j -> p c j i", i=4),
+                z_rows[:, :, cols].rearrange("p j (c i) -> p c j i", i=4),
             )
-        for cols in (slice(0, HALF), slice(HALF, S)):
+        for cols in halves:
             nc.vector.quantize_mx(
-                out=z_codes[:, cols].bitcast(FP8X4), scales=z_scales[:, cols], in_=z_grouped[:, cols, :].rearrange("p c j -> p (c j)")
+                out=z_codes[:, cols].bitcast(FP8X4),
+                scales=z_plane[:, cols],
+                in_=z_grouped[:, cols, :].rearrange("p c j -> p (c j)"),
             )
-        warm2 = sb("warm2", [P, 1], F32, tag="last")
-        nc.scalar.activation(warm2[:], half_t[:], ACT.Sigmoid, bias=half_t[:], scale=1.0)
-        quantize_w(1, nc.scalar.copy, "last")
+        warm_sigmoid = sbuf("warm_sigmoid", [P, 1], F32)
+        nc.scalar.activation(warm_sigmoid[:], h[3][:, 0:1], ACT.Sigmoid, bias=half_bias[:], scale=1.0)
+        quantize_w(1, nc.scalar.copy, tag="old_times3")
 
-        acc2 = [psum.tile([P, S], F32, name="acc_o%d" % m, tag="bank%d" % (PACK + m)) for m in range(PACK)]
-        sg = [sb("sg%d" % m, [P, S], F32) for m in range(PACK)]
-        res = [sb("res%d" % m, [P, S], F32) for m in range(PACK)]
-        passes = [(m, slice(HALF * u, HALF * (u + 1))) for u in range(2) for m in range(2)]
-        passes = passes + [(m, slice(0, S)) for m in range(2, PACK)]
+        acc_h2 = [psum.tile([P, S], F32, name="acc_h2_%d" % m, tag="bank%d" % (PACK + m)) for m in range(PACK)]
+        sg = [sbuf("sg%d" % m, [P, S], F32) for m in range(PACK)]
+        result = [sbuf("result%d" % m, [P, S], F32) for m in range(PACK)]
+        passes = [(m, cols) for cols in halves for m in range(2)] + [(m, slice(0, S)) for m in range(2, PACK)]
         for m, cols in passes:
-            rows = slice(P * m, P * (m + 1))
+            stationary = slice(P * m, P * (m + 1))
             nc.tensor.matmul_mx(
-                out=acc2[m][:, cols],
-                lhsT=w_codes[:, rows].bitcast(FP8X4),
-                lhsT_scale=w_scales[:, rows],
+                out=acc_h2[m][:, cols],
+                lhsT=w_codes[:, stationary].bitcast(FP8X4),
+                lhsT_scale=w_plane[:, stationary],
                 rhs=z_codes[:, cols].bitcast(FP8X4),
-                rhs_scale=z_scales[:, cols],
+                rhs_scale=z_plane[:, cols],
                 start=True,
                 stop=True,
             )
-        halves = [(slice(HALF * u, HALF * (u + 1)), slice(16 * u, 16 * (u + 1))) for u in range(2)]
-        out_rows = out.rearrange("(p t) c -> p t c", t=PACK)
 
-        def fetch_and_add(m, h2):
-            nc.vector.tensor_scalar(win[m][:, :S], h2, -1.0, None, ALU.mult)
-            nc.vector.tensor_tensor(st[m][:, :S], win[m][:].indirect(n3_t[:]), h2, ALU.add)
+        def difference_on_vector(m, h2):
+            nc.vector.tensor_scalar(n3_window[m][:, :S], h2, -1.0, None, ALU.mult)
+            nc.vector.tensor_tensor(st[m][:, :S], n3_window[m][:].indirect(n3_list[:]), h2, ALU.add)
 
-        def gate(m, cols, entries):
+        def gate(m, cols):
             nc.scalar.activation(
-                sg[m][:, cols], st[m][:].indirect(n4_t[:, entries]), ACT.Sigmoid, bias=bias[:, m : m + 1], scale=sl_t[:, m : m + 1]
+                sg[m][:, cols],
+                st[m][:].indirect(n4_list[:, entries(cols)]),
+                ACT.Sigmoid,
+                bias=bias[:, m : m + 1],
+                scale=sl_col[:, m : m + 1],
             )
 
-        def finish(m, cols):
-            nc.vector.tensor_tensor(res[m][:, cols], acc2[m][:, cols], sg[m][:, cols], ALU.mult)
-            nc.sync.dma_start(out_rows[:, m, cols], res[m][:, cols])
+        out_rows = out.rearrange("(p t) c -> p t c", t=PACK)
 
-        other = st[1][:, S:]
-        h2 = [st[m][:, S:] for m in range(PACK)]
-        nc.vector.tensor_copy(h2[0], acc2[0][:])
-        fetch_and_add(0, h2[0])
-        nc.scalar.copy(win[1][:, :S], acc2[1][:])
-        nc.scalar.activation(other, win[1][:].indirect(n3_t[:]), ACT.Copy)
-        nc.scalar.copy(h2[2], acc2[2][:])
-        nc.scalar.copy(h2[3], acc2[3][:])
-        nc.vector.tensor_tensor(st[1][:, :S], acc2[1][:], other, ALU.subtract)
-        fetch_and_add(2, h2[2])
-        fetch_and_add(3, h2[3])
-        for m in range(3):
-            gate(m, slice(0, S), slice(0, S // 16))
-        for cols, entries in halves:
-            gate(3, cols, entries)
-        for m in range(3):
-            finish(m, slice(0, S))
-        for cols, entries in halves:
-            finish(3, cols)
+        def finish(m, cols):
+            nc.vector.tensor_tensor(result[m][:, cols], acc_h2[m][:, cols], sg[m][:, cols], ALU.mult)
+            nc.sync.dma_start(out_rows[:, m, cols], result[m][:, cols])
+
+        h2_last = sbuf("h2_last", [P, S], F32)
+        nc.vector.tensor_copy(st[0][:, S:], acc_h2[0][:])
+        difference_on_vector(0, st[0][:, S:])
+        nc.scalar.copy(n3_window[1][:, :S], acc_h2[1][:])
+        nc.scalar.activation(st[1][:, S:], n3_window[1][:].indirect(n3_list[:]), ACT.Copy)
+        nc.scalar.copy(st[2][:, S:], acc_h2[2][:])
+        nc.scalar.copy(h2_last[:], acc_h2[last][:])
+        nc.vector.tensor_tensor(st[1][:, :S], acc_h2[1][:], st[1][:, S:], ALU.subtract)
+        difference_on_vector(2, st[2][:, S:])
+        difference_on_vector(last, h2_last[:])
+
+        quarter = S // 4
+        pieces = [(m, slice(0, S)) for m in range(last)]
+        pieces = pieces + [(last, cols) for cols in (halves[0], slice(HALF, HALF + quarter), slice(HALF + quarter, S))]
+        for m, cols in pieces:
+            gate(m, cols)
+        for m, cols in pieces:
+            finish(m, cols)

from contextlib import ExitStack

import concourse.mybir as mybir

F32 = mybir.dt.float32
BF16 = mybir.dt.bfloat16
I32 = mybir.dt.int32
U32 = mybir.dt.uint32
U16 = mybir.dt.uint16
U8 = mybir.dt.uint8
FP8X4 = mybir.dt.float8_e4m3fn_x4
ALU = mybir.AluOpType
ACT = mybir.ActivationFunctionType

P = 128
PACK = 4
QUADRANT = 32
BLOCK_PARTITIONS = 8
PLANE_START = 4
TABLE = 2048
S = 512
HALF = S // 2
W = 384
PER_COLUMN = 16
SPARE = 32
SIXTEENTH = 0.0625
FLOPS = 2 * 2 * S * S * S


def tile_picked_pqlayknormehq_none_p_kernel(
    tc, x_words, x_scales, d_words, d_scales, gn, w1, sl, th, offs, k1, n1, n2, n3, n4, out
):
    nc = tc.nc
    halves = [slice(0, HALF), slice(HALF, S)]

    with ExitStack() as ctx:
        keep = ctx.enter_context(tc.tile_pool(name="keep", bufs=1))
        psum = ctx.enter_context(tc.psum_pool(name="psum", bufs=1))

        def sbuf(name, shape, dtype, tag=None):
            return keep.tile(shape, dtype, name=name, tag=tag or name, align_bytes=64)

        def load_list(name, source):
            tile = keep.tile(list(source.shape), U16, name=name)
            nc.sync.dma_start(tile[:], source)
            return tile

        def load_scale_rows(tile, scales):
            rows = scales[0].bitcast(I32).unsqueeze(1)
            nc.sync.dma_start(tile[:].bitcast(I32), rows.broadcast_to([P // BLOCK_PARTITIONS, BLOCK_PARTITIONS, TABLE // 4]))

        def load_words(tile, words):
            nc.sync.dma_start(tile[:], words[0].rearrange("p n t -> p (n t)").bitcast(I32))

        def entries(cols):
            return slice(cols.start // PER_COLUMN, cols.stop // PER_COLUMN)

        def deal(target, source):
            nc.vector.tensor_copy(
                target.rearrange("p (t m) -> p m t", t=PACK), source.rearrange("p (m t) -> p m t", t=PACK)
            )

        half_bias = sbuf("half_bias", [P, 1], F32)
        nc.vector.memset(half_bias[:], 0.5)
        warm_root = sbuf("warm_root", [P, 1], F32)
        nc.scalar.activation(warm_root[:], half_bias[:], ACT.Abs_reciprocal_sqrt, bias=half_bias[:], scale=SIXTEENTH)

        d_scale_table = sbuf("d_scale_table", [P, TABLE], U8)
        x_scale_table = sbuf("x_scale_table", [P, TABLE], U8)
        d_word_table = sbuf("d_word_table", [P, TABLE], I32)
        x_word_table = sbuf("x_word_table", [P, TABLE], I32)
        k1_list = load_list("k1_list", k1)
        load_scale_rows(d_scale_table, d_scales)
        offs_list = load_list("offs_list", offs)
        load_scale_rows(x_scale_table, x_scales)
        load_words(d_word_table, d_words)
        n2_list = load_list("n2_list", n2)
        n1_list = load_list("n1_list", n1)
        n3_list = load_list("n3_list", n3)
        load_words(x_word_table, x_words)
        n4_list = load_list("n4_list", n4)

        d_scale_picked = sbuf("d_scale_picked", [P, S], U8)
        x_scale_picked = sbuf("x_scale_picked", [P, S], U8)
        planes = sbuf("planes", [P, 2 * S], U8)
        nc.vector.tensor_copy(d_scale_picked[:], d_scale_table[:].indirect(k1_list[:]))
        nc.vector.tensor_copy(x_scale_picked[:], x_scale_table[:].indirect(offs_list[:]))
        deal(planes[:, S:], d_scale_picked[:])
        nc.vector.tensor_copy(planes[:, :S].bitcast(I32), x_scale_picked[:].bitcast(I32))
        for i in range(1, QUADRANT // BLOCK_PARTITIONS):
            nc.scalar.dma_start(
                planes[PLANE_START + i : P : QUADRANT, :].bitcast(I32),
                planes[BLOCK_PARTITIONS * i : P : QUADRANT, :].bitcast(I32),
            )

        d_word_picked = sbuf("d_word_picked", [P, S], U32)
        d_codes = sbuf("d_codes", [P, S], U32)
        x_codes = sbuf("x_codes", [P, S], U32)
        nc.vector.tensor_copy(d_word_picked[:], d_word_table[:].bitcast(U32).indirect(k1_list[:]))
        deal(d_codes[:], d_word_picked[:])
        for cols in halves:
            nc.vector.tensor_copy(x_codes[:, cols], x_word_table[:].bitcast(U32).indirect(offs_list[:, entries(cols)]))

        vectors = sbuf("vectors", [P, 3, 2 * PACK], F32, tag="d_word_picked")
        gn_col, sl_col, th_col = (vectors[:, i, :PACK] for i in range(3))
        for target, source in ((gn_col, gn), (sl_col, sl), (th_col, th)):
            nc.sync.dma_start(target, source[:, 0].rearrange("(p t) -> p t", t=PACK))
        w_raw = sbuf("w_raw", [P, PACK, S], F32, tag="x_word_table")
        nc.sync.dma_start(w_raw[:], w1.rearrange("(p j) c -> p j c", j=PACK))

        last = PACK - 1
        n3_window = [sbuf("n3_window%d" % m, [P, S + SPARE], F32) for m in range(PACK)]
        st = [sbuf("st%d" % m, [P, S if m == last else 2 * S], F32) for m in range(PACK)]
        for m in range(PACK):
            nc.vector.memset(n3_window[m][:, S:], 0.0)

        h = [sbuf("h%d" % t, [P, S], F32) for t in range(PACK)]

        def first_product(t, cols, bank):
            acc = psum.tile([P, cols.stop - cols.start], F32, name="acc_h%d_%d" % (t, bank), tag="bank%d" % bank)
            nc.tensor.matmul_mx(
                out=acc[:],
                lhsT=d_codes[:, P * t : P * (t + 1)].bitcast(FP8X4),
                lhsT_scale=planes[PLANE_START:, S + P * t : S + P * (t + 1)],
                rhs=x_codes[:, cols].bitcast(FP8X4),
                rhs_scale=planes[PLANE_START:, cols],
                start=True,
                stop=True,
            )
            nc.scalar.copy(h[t][:, cols], acc[:])

        for t in range(2):
            first_product(t, halves[0], PACK + t)
        for t in range(2):
            first_product(t, halves[1], t)
        for t in range(2, PACK):
            first_product(t, slice(0, S), t)

        def inverse_root(magnitude, name):
            root = sbuf(name, list(magnitude.shape), F32)
            nc.scalar.activation(root[:], magnitude[:], ACT.Abs_reciprocal_sqrt, bias=half_bias[:], scale=SIXTEENTH)
            return root

        def magnitude_on_scalar(tiles, name):
            pa = sbuf("pa" + name, [P, len(tiles) * W], F32)
            magnitude = sbuf("magnitude" + name, [P, len(tiles) * W], F32)
            for i, t in enumerate(tiles):
                nc.scalar.activation(pa[:, W * i : W * (i + 1)], h[t][:].indirect(n2_list[:]), ACT.Copy)
            nc.scalar.activation(magnitude[:], pa[:], ACT.Abs)
            return magnitude

        def squared(root, name):
            square = sbuf(name, list(root.shape), F32)
            nc.scalar.activation(square[:], root[:], ACT.Square)
            return square

        def fetch_old(t, tag=None):
            old = sbuf("old%d" % t, [P, W], F32, tag=tag)
            nc.vector.tensor_copy(old[:], h[t][:].indirect(n1_list[:]))
            return old

        def fetch_old_times(t, factor):
            product = sbuf("old_times%d" % t, [P, W], F32)
            nc.vector.tensor_tensor(product[:], h[t][:].indirect(n1_list[:]), factor, ALU.mult)
            return product

        def put_back(t, values, factor):
            nc.vector.tensor_tensor(h[t][:].indirect(n1_list[:]), values[:], factor, ALU.mult)

        w_codes = sbuf("w_codes", [P, S], U32)
        w_plane = sbuf("w_plane", [P, S], U8)
        w_dealt = w_raw[:].rearrange("p j (m t) -> p m j t", t=PACK)

        def quantize_w(u, copy, tag=None):
            grouped = sbuf("w_grouped%d" % u, [P, HALF, PACK], BF16, tag=tag)
            copy(grouped[:].rearrange("p (t m) j -> p m j t", t=2), w_dealt[:, :, :, 2 * u : 2 * u + 2])
            nc.vector.quantize_mx(
                out=w_codes[:, halves[u]].bitcast(FP8X4),
                scales=w_plane[:, halves[u]],
                in_=grouped[:].rearrange("p c j -> p (c j)"),
            )

        pa0 = sbuf("pa0", [P, W], F32)
        magnitude0 = sbuf("magnitude0", [P, W], F32)
        nc.vector.tensor_copy(pa0[:], h[0][:].indirect(n2_list[:]))
        nc.vector.scalar_tensor_tensor(magnitude0[:], pa0[:], -1.0, pa0[:], ALU.mult, ALU.max)
        reciprocal0 = squared(inverse_root(magnitude0, "root0"), "reciprocal0")
        old0 = fetch_old(0, tag="pa0")
        gain = sbuf("gain", [P, PACK], F32, tag="root0")
        bias = sbuf("bias", [P, PACK], F32, tag="magnitude0")
        nc.vector.tensor_scalar(gain[:], gn_col, SIXTEENTH, None, ALU.mult)
        nc.vector.scalar_tensor_tensor(bias[:], sl_col, -1.0, th_col, ALU.mult, ALU.mult)
        root1 = inverse_root(magnitude_on_scalar([1], "1"), "root1")
        reciprocal23 = squared(inverse_root(magnitude_on_scalar([2, 3], "23"), "root23"), "reciprocal23")
        put_back(0, old0, reciprocal0[:])
        put_back(1, fetch_old_times(1, root1[:]), root1[:])
        ra3 = fetch_old_times(3, reciprocal23[:, W:])
        put_back(2, fetch_old(2), reciprocal23[:, :W])
        quantize_w(0, nc.vector.tensor_copy)

        z_rows = sbuf("z_rows", [P, PACK, S], BF16, tag="root23")
        for t in range(2):
            nc.scalar.activation(z_rows[:, t, :], h[t][:], ACT.Copy, scale=gain[:, t : t + 1])
        nc.scalar.activation(h[3][:].indirect(n1_list[:]), ra3[:], ACT.Copy)
        for t in range(2, PACK):
            nc.vector.tensor_scalar(z_rows[:, t, :], h[t][:], gain[:, t : t + 1], None, ALU.mult)

        z_grouped = sbuf("z_grouped", [P, S, PACK], BF16)
        z_codes = sbuf("z_codes", [P, S], U32)
        z_plane = sbuf("z_plane", [P, S], U8)
        for cols in halves:
            nc.vector.tensor_copy(
                z_grouped[:, cols, :].rearrange("p (c i) j -> p c j i", i=4),
                z_rows[:, :, cols].rearrange("p j (c i) -> p c j i", i=4),
            )
        for cols in halves:
            nc.vector.quantize_mx(
                out=z_codes[:, cols].bitcast(FP8X4),
                scales=z_plane[:, cols],
                in_=z_grouped[:, cols, :].rearrange("p c j -> p (c j)"),
            )
        warm_sigmoid = sbuf("warm_sigmoid", [P, 1], F32)
        nc.scalar.activation(warm_sigmoid[:], h[3][:, 0:1], ACT.Sigmoid, bias=half_bias[:], scale=1.0)
        quantize_w(1, nc.scalar.copy, tag="old_times3")

        acc_h2 = [psum.tile([P, S], F32, name="acc_h2_%d" % m, tag="bank%d" % (PACK + m)) for m in range(PACK)]
        sg = [sbuf("sg%d" % m, [P, S], F32) for m in range(PACK)]
        result = [sbuf("result%d" % m, [P, S], F32) for m in range(PACK)]
        passes = [(m, cols) for cols in halves for m in range(2)] + [(m, slice(0, S)) for m in range(2, PACK)]
        for m, cols in passes:
            stationary = slice(P * m, P * (m + 1))
            nc.tensor.matmul_mx(
                out=acc_h2[m][:, cols],
                lhsT=w_codes[:, stationary].bitcast(FP8X4),
                lhsT_scale=w_plane[:, stationary],
                rhs=z_codes[:, cols].bitcast(FP8X4),
                rhs_scale=z_plane[:, cols],
                start=True,
                stop=True,
            )

        def difference_on_vector(m, h2):
            nc.vector.tensor_scalar(n3_window[m][:, :S], h2, -1.0, None, ALU.mult)
            nc.vector.tensor_tensor(st[m][:, :S], n3_window[m][:].indirect(n3_list[:]), h2, ALU.add)

        def gate(m, cols):
            nc.scalar.activation(
                sg[m][:, cols],
                st[m][:].indirect(n4_list[:, entries(cols)]),
                ACT.Sigmoid,
                bias=bias[:, m : m + 1],
                scale=sl_col[:, m : m + 1],
            )

        out_rows = out.rearrange("(p t) c -> p t c", t=PACK)

        def finish(m, cols):
            nc.vector.tensor_tensor(result[m][:, cols], acc_h2[m][:, cols], sg[m][:, cols], ALU.mult)
            nc.sync.dma_start(out_rows[:, m, cols], result[m][:, cols])

        h2_last = sbuf("h2_last", [P, S], F32)
        nc.vector.tensor_copy(st[0][:, S:], acc_h2[0][:])
        difference_on_vector(0, st[0][:, S:])
        nc.scalar.copy(n3_window[1][:, :S], acc_h2[1][:])
        nc.scalar.activation(st[1][:, S:], n3_window[1][:].indirect(n3_list[:]), ACT.Copy)
        nc.scalar.copy(st[2][:, S:], acc_h2[2][:])
        nc.scalar.copy(h2_last[:], acc_h2[last][:])
        nc.vector.tensor_tensor(st[1][:, :S], acc_h2[1][:], st[1][:, S:], ALU.subtract)
        difference_on_vector(2, st[2][:, S:])
        difference_on_vector(last, h2_last[:])

        quarter = S // 4
        pieces = [(m, slice(0, S)) for m in range(last)]
        pieces = pieces + [(last, cols) for cols in (halves[0], slice(HALF, HALF + quarter), slice(HALF + quarter, S))]
        for m, cols in pieces:
            gate(m, cols)
        for m, cols in pieces:
            finish(m, cols)
